import numpy as np
import ml_dtypes


def mxq(x, axis, fmt="e4m3"):
    dtype, down = {"e4m3": (ml_dtypes.float8_e4m3fn, 7), "e5m2": (ml_dtypes.float8_e5m2, 14)}[fmt]
    v = np.moveaxis(np.asarray(x, np.float32).astype(ml_dtypes.bfloat16).astype(np.float64), axis, -1)
    blocks = v.reshape(v.shape[:-1] + (-1, 32))
    amax = np.abs(blocks).max(-1, keepdims=True)
    byte = np.maximum(np.where(amax > 0, np.frexp(amax)[1] - 1 + 127, 0) - down, 1)
    scale = np.exp2(byte - 127.0)
    codes = (blocks / scale).astype(np.float32).astype(dtype).astype(np.float64)
    return np.moveaxis((codes * scale).reshape(v.shape), -1, axis)


WIDE = False


def mx_kscale(k):
    if not WIDE:
        return np.ones(k)
    levels = np.array([10, -10, 5, -5, 0])
    if k % 512:
        return np.exp2(np.random.permutation(np.resize(levels, k // 32))).repeat(32)
    a = np.empty((k // 512, 16))
    for p in range(k // 512):
        a[p, :8] = np.random.permutation(np.resize(levels, 8))
        for g in range(8):
            far = levels[np.abs(levels - a[p, g]) >= 10]
            a[p, g + 8] = far[np.random.randint(len(far))]
    return np.exp2(a.ravel()).repeat(32)


def f64(x):
    return np.asarray(x).astype(np.float64)


def striped(idx):
    return np.tile(idx.reshape(-1, 16).T, (8, 1)).astype(np.uint16)


def unstriped(offs):
    return offs[:16].T.reshape(-1).astype(np.int64)


def striped8(idx):
    return np.concatenate([x.reshape(-1, 16).T for x in idx]).astype(np.uint16)


def runs(offs, k):
    lists = np.stack([offs[16 * r : 16 * r + 16].T.reshape(-1) for r in range(8)]).astype(np.int64)
    return lists[np.arange(k) % 512 // 64]


def pack_weight(w):
    k, n = w.shape
    w = f64(np.asarray(w, np.float32).astype(ml_dtypes.bfloat16)).reshape(k // 32, 32, n)
    amax = np.abs(w).max(1)
    byte = np.clip(np.where(amax > 0, np.frexp(amax)[1] - 1 + 127 - 7, 1), 1, 254)
    scaled = (w * np.exp2(127.0 - byte)[:, None, :]).reshape(k, n).astype(np.float32)
    words = np.ascontiguousarray(scaled.reshape(k // 512, 128, 4, n).transpose(0, 1, 3, 2)).astype(ml_dtypes.float8_e4m3fn).view(np.uint8)
    return words, np.ascontiguousarray(byte.astype(np.uint8).reshape(k // 512, 16, n))


def unpack_weight(words, scales):
    g, p, n, _ = words.shape
    vals = np.ascontiguousarray(words).view(ml_dtypes.float8_e4m3fn).astype(np.float64) * np.repeat(np.exp2(scales.astype(np.float64) - 127.0), 8, axis=1)[..., None]
    return vals.transpose(0, 1, 3, 2).reshape(g * 512, n)

def planes(y):
    n, m = y.shape
    v = y.astype(np.float32).astype(ml_dtypes.bfloat16).astype(np.float64).reshape(n // 32, 32, m)
    top = np.abs(v).max(1)
    byte = np.clip(np.where(top > 0, np.frexp(top)[1] - 1 + 127 - 7, 1), 1, 254)
    codes = (v * np.exp2(127.0 - byte)[:, None, :]).reshape(n, m).astype(np.float32).astype(ml_dtypes.float8_e4m3fn).view(np.uint8)
    words = codes.reshape(n // 512, 128, 4, m).transpose(0, 1, 3, 2)
    return np.ascontiguousarray(words), np.ascontiguousarray(byte.astype(np.uint8).reshape(n // 512, 16, m))


K, T, S, G, H = 512, 1024, 512, 2048, 512


def setup_inputs():
    n = np.random.standard_normal
    s = mx_kscale(K)[:, None]
    packed_xT = pack_weight(n((K, T)) * s)
    packed_dT = pack_weight(n((K, G)) / s)
    return {
        "x_words": packed_xT[0],
        "x_scales": packed_xT[1],
        "d_words": packed_dT[0],
        "d_scales": packed_dT[1],
        "gs": (np.random.uniform(0.5, 1.5, (K, 1)) * s).astype(np.float32),
        "offs": striped(np.random.permutation(T)[:S]),
        "k1": striped8(np.random.randint(0, G, (8, H))),
        "n1": striped8(np.stack([np.random.permutation(S) for _ in range(8)])),
        "n2": striped8(np.stack([np.random.permutation(S) for _ in range(8)])),
        "k2": striped8(np.random.randint(0, G, (8, H))),
        "n3": striped8(np.stack([np.random.permutation(S) for _ in range(8)])),
    }


def reference(x_words, x_scales, d_words, d_scales, gs, offs, k1, n1, n2, k2, n3):
    d_k2 = unpack_weight(d_words, d_scales)[np.arange(K)[:, None], runs(k2, K)]
    d_k1 = unpack_weight(d_words, d_scales)[np.arange(K)[:, None], runs(k1, K)]
    xq = unpack_weight(x_words, x_scales)[:, unstriped(offs)]
    h = 0.0625 * (d_k1.T @ xq)
    sq = (h) ** 2
    z = f64(gs) * ((h[np.arange(H)[:, None], runs(n2, H)]) / (np.sqrt(sq + sq[np.arange(H)[:, None], runs(n1, H)] + 0.25)))
    h2 = 0.0625 * ((d_k2.T @ mxq(z, 0, "e4m3")))
    pa = h2[np.arange(H)[:, None], runs(n3, H)]
    out_0 = (2.0 * (h2 * pa)) / ((h2) ** 2 + (pa) ** 2 + 0.5)
    return (out_0,) + planes(out_0)

@@ -1,0 +1,246 @@
+from contextlib import ExitStack
+
+import concourse.mybir as mybir
+
+F32 = mybir.dt.float32
+BF16 = mybir.dt.bfloat16
+I32 = mybir.dt.int32
+U32 = mybir.dt.uint32
+U16 = mybir.dt.uint16
+U8 = mybir.dt.uint8
+FP8X4 = mybir.dt.float8_e4m3fn_x4
+ACT = mybir.ActivationFunctionType
+ALU = mybir.AluOpType
+
+P = 128
+PACK = 4
+K, T, S, G, H = 512, 1024, 512, 2048, 512
+HALF = S // 2
+LANES = 16
+FLOPS = 2 * 2 * K * H * S
+
+
+def tile_picked_codermsharm_none_po_kernel(
+    tc, x_words, x_scales, d_words, d_scales, gs, offs, k1, n1, n2, k2, n3, out_0, out_1, out_2
+):
+    nc = tc.nc
+    with ExitStack() as ctx:
+        keep = ctx.enter_context(tc.tile_pool(name="keep", bufs=1))
+        psum = ctx.enter_context(tc.psum_pool(name="psum", bufs=1))
+
+        def sb(name, shape, dtype):
+            return keep.tile(shape, dtype, name=name, align_bytes=64)
+
+        def load_list(name, src):
+            lst = keep.tile([P, S // LANES], U16, name=name)
+            nc.sync.dma_start(lst[:], src)
+            return lst
+
+        def half_of(lst, c):
+            return lst[:, c * HALF // LANES : (c + 1) * HALF // LANES]
+
+        d_bytes = sb("d_bytes", [P, G], U8)
+        x_bytes = sb("x_bytes", [P, T], U8)
+        nc.gpsimd.memset(d_bytes[:].bitcast(I32), 0)
+        nc.vector.memset(x_bytes[:].bitcast(I32), 0)
+        nc.scalar.dma_start(d_bytes[0:P:8, :].bitcast(I32), d_scales[0].bitcast(I32))
+        nc.scalar.dma_start(x_bytes[0:P:8, :].bitcast(I32), x_scales[0].bitcast(I32))
+
+        warm_in = sb("warm_in", [P, 1], F32)
+        warm_out = sb("warm_out", [P, 1], F32)
+        nc.vector.memset(warm_in[:], 1.0)
+        nc.scalar.activation(warm_out[:], warm_in[:], ACT.Abs_reciprocal_sqrt)
+
+        k1_l = load_list("k1_l", k1)
+        offs_l = load_list("offs_l", offs)
+        x_tab = sb("x_tab", [P, T], U32)
+        d_tab = sb("d_tab", [P, G], U32)
+        nc.sync.dma_start(x_tab[:].bitcast(I32), x_words[0].rearrange("p n t -> p (n t)").bitcast(I32))
+        nc.sync.dma_start(d_tab[:].bitcast(I32), d_words[0].rearrange("p n t -> p (n t)").bitcast(I32))
+        k2_l = load_list("k2_l", k2)
+        n1_l = load_list("n1_l", n1)
+        gs_t = sb("gs_t", [P, PACK], F32)
+        nc.sync.dma_start(gs_t[:], gs.rearrange("(p t) o -> p (t o)", t=PACK))
+        n2_l = load_list("n2_l", n2)
+        n3_l = load_list("n3_l", n3)
+
+        plane1 = sb("plane1", [P, H + S], U8)
+        plane2 = sb("plane2", [P, H], U8)
+        nc.gpsimd.memset(plane1[:].bitcast(I32), 0)
+        nc.gpsimd.memset(plane2[:].bitcast(I32), 0)
+
+        def pick_bytes(name, table, lst):
+            got = sb(name, [P, S], U8)
+            nc.vector.tensor_copy(got[:], table[:].indirect(lst[:]))
+            return got
+
+        def deal_bytes(dst, got):
+            nc.vector.tensor_copy(dst.rearrange("p (t m) -> p t m", t=PACK), got[:].rearrange("p (m t) -> p t m", t=PACK))
+
+        def settle_rows(plane, spread):
+            for q in range(4):
+                nc.sync.dma_start(plane[32 * q : 32 * q + 4, :].bitcast(I32), spread[32 * q : 32 * q + 32 : 8, :].bitcast(I32))
+
+        def pick_weights(name, lst):
+            got = sb(name + "_got", [P, H], U32)
+            nc.vector.tensor_copy(got[:], d_tab[:].indirect(lst[:]))
+            dealt = sb(name, [P, H], U32)
+            nc.vector.tensor_copy(
+                dealt[:].rearrange("p (t b i) -> p b t i", t=PACK, i=4),
+                got[:].rearrange("p (b i t) -> p b t i", t=PACK, i=4),
+            )
+            return dealt
+
+        def interleave(engine_copy, dst, src):
+            engine_copy(dst[:].rearrange("p (c i) t -> p c t i", i=4), src[:].rearrange("p t (c i) -> p c t i", i=4))
+
+        w1_bytes = pick_bytes("w1_bytes", d_bytes, k1_l)
+        xq_bytes = pick_bytes("xq_bytes", x_bytes, offs_l)
+        spread1 = sb("spread1", [P, H + S], U8)
+        deal_bytes(spread1[:, 0:H], w1_bytes)
+        nc.vector.tensor_copy(spread1[:, H : H + S].bitcast(I32), xq_bytes[:].bitcast(I32))
+        settle_rows(plane1, spread1)
+        xq = sb("xq", [P, S], U32)
+        nc.vector.tensor_copy(xq[:], x_tab[:].indirect(offs_l[:]))
+        w1 = pick_weights("w1", k1_l)
+
+        h_ps = [psum.tile([P, S], F32, name="h_ps%d" % t) for t in range(PACK)]
+        for t in range(PACK):
+            cols = slice(t * P, (t + 1) * P)
+            nc.tensor.matmul_mx(
+                out=h_ps[t][:], lhsT=w1[:, cols].bitcast(FP8X4), lhsT_scale=plane1[:, cols],
+                rhs=xq[:].bitcast(FP8X4), rhs_scale=plane1[:, H : H + S], start=True, stop=True,
+            )
+
+        w2_bytes = pick_bytes("w2_bytes", d_bytes, k2_l)
+        spread2 = sb("spread2", [P, H], U8)
+        deal_bytes(spread2[:], w2_bytes)
+        settle_rows(plane2, spread2)
+        w2 = pick_weights("w2", k2_l)
+
+        sq = [sb("sq%d" % t, [P, S], F32) for t in range(PACK)]
+        sq_own = [sb("sq_own%d" % t, [P, S], F32) for t in range(PACK)]
+        hg = [sb("hg%d" % t, [P, S], F32) for t in range(PACK)]
+        ssum = [sb("ssum%d" % t, [P, S], F32) for t in range(PACK)]
+        rinv = [sb("rinv%d" % t, [P, S], F32) for t in range(PACK)]
+        z = [sb("z%d" % c, [P, PACK, HALF], F32) for c in range(2)]
+
+        def fetch_z(t, c):
+            cols = slice(c * HALF, (c + 1) * HALF)
+            nc.vector.tensor_tensor(z[c][:, t, :], hg[t][:].indirect(half_of(n2_l, c)), rinv[t][:, cols], ALU.mult)
+
+        def root_of(t, c):
+            cols = slice(c * HALF, (c + 1) * HALF)
+            nc.scalar.activation(rinv[t][:, cols], ssum[t][:, cols], ACT.Abs_reciprocal_sqrt, scale=256.0, bias=64.0)
+
+        for t in range(PACK):
+            nc.scalar.activation(sq[t][:], h_ps[t][:], ACT.Square, scale=0.0625)
+            nc.scalar.activation(sq_own[t][:], h_ps[t][:], ACT.Square, scale=0.0625)
+            for c in range(2):
+                cols = slice(c * HALF, (c + 1) * HALF)
+                nc.vector.tensor_tensor(ssum[t][:, cols], sq[t][:].indirect(half_of(n1_l, c)), sq_own[t][:, cols], ALU.add)
+        for t in range(PACK):
+            nc.scalar.activation(hg[t][:], h_ps[t][:], ACT.Copy, scale=gs_t[:, t : t + 1])
+            root_of(t, 0)
+            fetch_z(t, 0)
+        for t in range(PACK):
+            root_of(t, 1)
+
+        zq = sb("zq", [P, S], U32)
+        zq_bytes = sb("zq_bytes", [P, S], U8)
+        h2_ps = [[psum.tile([P, 2, HALF], F32, name="h2_ps%d%d" % (c, u)) for u in range(2)] for c in range(2)]
+        h2 = [sb("h2_%d" % t, [P, S], F32) for t in range(PACK)]
+        h2_sq = [[sb("h2_sq%d%d" % (c, u), [P, 2, HALF], F32) for u in range(2)] for c in range(2)]
+
+        def second_layer(c, z_bf):
+            cols = slice(c * HALF, (c + 1) * HALF)
+            nc.vector.quantize_mx(out=zq[:, cols].bitcast(FP8X4), scales=zq_bytes[:, cols], in_=z_bf[:].rearrange("p c t -> p (c t)"))
+            for t in range(PACK):
+                rows = slice(t * P, (t + 1) * P)
+                nc.tensor.matmul_mx(
+                    out=h2_ps[c][t // 2][:, t % 2, :], lhsT=w2[:, rows].bitcast(FP8X4), lhsT_scale=plane2[:, rows],
+                    rhs=zq[:, cols].bitcast(FP8X4), rhs_scale=zq_bytes[:, cols], start=True, stop=True,
+                )
+
+        def h2_out(c, t):
+            cols = slice(c * HALF, (c + 1) * HALF)
+            if c == 0:
+                nc.vector.tensor_scalar(h2[t][:, cols], h2_ps[c][t // 2][:, t % 2, :], 0.0625, None, ALU.mult)
+            else:
+                nc.scalar.activation(h2[t][:, cols], h2_ps[c][t // 2][:, t % 2, :], ACT.Copy, scale=0.0625)
+
+        z_bf = [sb("z_bf%d" % c, [P, HALF, PACK], BF16) for c in range(2)]
+        interleave(nc.scalar.copy, z_bf[0], z[0])
+        for t in range(PACK - 1):
+            fetch_z(t, 1)
+        second_layer(0, z_bf[0])
+        fetch_z(PACK - 1, 1)
+        interleave(nc.vector.tensor_copy, z_bf[1], z[1])
+        h2_out(0, 0)
+        second_layer(1, z_bf[1])
+        for t in range(1, PACK):
+            h2_out(0, t)
+        nc.scalar.activation(h2_sq[0][0][:], h2_ps[0][0][:], ACT.Square, scale=0.0625)
+        for t in range(PACK):
+            h2_out(1, t)
+        nc.scalar.activation(h2_sq[0][1][:], h2_ps[0][1][:], ACT.Square, scale=0.0625)
+
+        units = [(c, u) for c in range(2) for u in range(2)]
+        pa = {k: sb("pa%d%d" % k, [P, 2, HALF], F32) for k in units}
+        pa_sq = {k: sb("pa_sq%d%d" % k, [P, 2, HALF], F32) for k in units}
+        den = {k: sb("den%d%d" % k, [P, 2, HALF], F32) for k in units}
+        root = {k: sb("root%d%d" % k, [P, 2, HALF], F32) for k in units}
+        inv = {k: sb("inv%d%d" % k, [P, 2, HALF], F32) for k in units}
+        num = {k: sb("num%d%d" % k, [P, 2, HALF], F32) for k in units}
+        y = [sb("y%d" % c, [P, PACK, HALF], F32) for c in range(2)]
+        y_bf = [sb("y_bf%d" % c, [P, HALF, PACK], BF16) for c in range(2)]
+        yq = sb("yq", [P, S], U32)
+        yq_bytes = sb("yq_bytes", [P, S], U8)
+        out_rows = out_0.rearrange("(p t) c -> p t c", t=PACK)
+        out_words = out_1[0].rearrange("p n t -> p (n t)").bitcast(I32)
+
+        def fetch(k):
+            c, u = k
+            for i in range(2):
+                nc.vector.tensor_copy(pa[k][:, i, :], h2[2 * u + i][:].indirect(half_of(n3_l, c)))
+            nc.scalar.activation(pa_sq[k][:], pa[k][:], ACT.Square)
+            if c == 1:
+                nc.scalar.activation(h2_sq[c][u][:], h2_ps[c][u][:], ACT.Square, scale=0.0625)
+
+        def middle(k):
+            c, u = k
+            nc.vector.tensor_tensor(den[k][:], pa_sq[k][:], h2_sq[c][u][:], ALU.add)
+            nc.scalar.activation(root[k][:], den[k][:], ACT.Abs_reciprocal_sqrt, bias=0.5)
+            nc.scalar.activation(inv[k][:], root[k][:], ACT.Square)
+            nc.vector.scalar_tensor_tensor(num[k][:], h2_ps[c][u][:], 0.125, pa[k][:], ALU.mult, ALU.mult)
+
+        def finish(k):
+            c, u = k
+            cols = slice(c * HALF, (c + 1) * HALF)
+            nc.vector.tensor_tensor(y[c][:, 2 * u : 2 * u + 2, :], num[k][:], inv[k][:], ALU.mult)
+            nc.sync.dma_start(out_rows[:, 2 * u : 2 * u + 2, cols], y[c][:, 2 * u : 2 * u + 2, :])
+
+        def hand_on(c):
+            cols = slice(c * HALF, (c + 1) * HALF)
+            nc.vector.quantize_mx(out=yq[:, cols].bitcast(FP8X4), scales=yq_bytes[:, cols], in_=y_bf[c][:].rearrange("p c t -> p (c t)"))
+            nc.sync.dma_start(out_words[:, cols], yq[:, cols].bitcast(I32))
+
+        fetch(units[0])
+        fetch(units[1])
+        middle(units[0])
+        fetch(units[2])
+        middle(units[1])
+        finish(units[0])
+        fetch(units[3])
+        middle(units[2])
+        finish(units[1])
+        middle(units[3])
+        interleave(nc.scalar.copy, y_bf[0], y[0])
+        finish(units[2])
+        finish(units[3])
+        hand_on(0)
+        interleave(nc.vector.tensor_copy, y_bf[1], y[1])
+        hand_on(1)
+        for q in range(4):
+            queue = nc.sync if q % 2 == 0 else nc.scalar
+            queue.dma_start(out_2[0, 4 * q : 4 * q + 4, :].bitcast(I32), yq_bytes[32 * q : 32 * q + 4, :].bitcast(I32))

@@ -1,6 +1,7 @@
 from contextlib import ExitStack
 
 import concourse.mybir as mybir
+from concourse.masks import make_identity
 
 F32 = mybir.dt.float32
 BF16 = mybir.dt.bfloat16
@@ -43,8 +44,6 @@ def tile_picked_codermsharm_none_po_kernel(
         x_bytes = sb("x_bytes", [P, T], U8)
         nc.gpsimd.memset(d_bytes[:].bitcast(I32), 0)
         nc.vector.memset(x_bytes[:].bitcast(I32), 0)
-        nc.scalar.dma_start(d_bytes[0:P:8, :].bitcast(I32), d_scales[0].bitcast(I32))
-        nc.scalar.dma_start(x_bytes[0:P:8, :].bitcast(I32), x_scales[0].bitcast(I32))
 
         warm_in = sb("warm_in", [P, 1], F32)
         warm_out = sb("warm_out", [P, 1], F32)
@@ -53,21 +52,25 @@ def tile_picked_codermsharm_none_po_kernel(
 
         k1_l = load_list("k1_l", k1)
         offs_l = load_list("offs_l", offs)
+        nc.sync.dma_start(d_bytes[0:P:8, :].bitcast(I32), d_scales[0].bitcast(I32))
+        nc.sync.dma_start(x_bytes[0:P:8, :].bitcast(I32), x_scales[0].bitcast(I32))
         x_tab = sb("x_tab", [P, T], U32)
         d_tab = sb("d_tab", [P, G], U32)
         nc.sync.dma_start(x_tab[:].bitcast(I32), x_words[0].rearrange("p n t -> p (n t)").bitcast(I32))
         nc.sync.dma_start(d_tab[:].bitcast(I32), d_words[0].rearrange("p n t -> p (n t)").bitcast(I32))
-        k2_l = load_list("k2_l", k2)
         n1_l = load_list("n1_l", n1)
         gs_t = sb("gs_t", [P, PACK], F32)
         nc.sync.dma_start(gs_t[:], gs.rearrange("(p t) o -> p (t o)", t=PACK))
         n2_l = load_list("n2_l", n2)
         n3_l = load_list("n3_l", n3)
+        k2_l = load_list("k2_l", k2)
 
         plane1 = sb("plane1", [P, H + S], U8)
         plane2 = sb("plane2", [P, H], U8)
         nc.gpsimd.memset(plane1[:].bitcast(I32), 0)
         nc.gpsimd.memset(plane2[:].bitcast(I32), 0)
+        ident = sb("ident", [P, P], F32)
+        make_identity(nc, ident[:])
 
         def pick_bytes(name, table, lst):
             got = sb(name, [P, S], U8)
@@ -92,7 +95,7 @@ def tile_picked_codermsharm_none_po_kernel(
             return dealt
 
         def interleave(engine_copy, dst, src):
-            engine_copy(dst[:].rearrange("p (c i) t -> p c t i", i=4), src[:].rearrange("p t (c i) -> p c t i", i=4))
+            engine_copy(dst[:].rearrange("p (c i) t -> p c t i", i=4), src.rearrange("p t (c i) -> p c t i", i=4))
 
         w1_bytes = pick_bytes("w1_bytes", d_bytes, k1_l)
         xq_bytes = pick_bytes("xq_bytes", x_bytes, offs_l)
@@ -104,7 +107,7 @@ def tile_picked_codermsharm_none_po_kernel(
         nc.vector.tensor_copy(xq[:], x_tab[:].indirect(offs_l[:]))
         w1 = pick_weights("w1", k1_l)
 
-        h_ps = [psum.tile([P, S], F32, name="h_ps%d" % t) for t in range(PACK)]
+        h_ps = [psum.tile([P, S], F32, name="h_ps%d" % t, tag="bank%d" % t) for t in range(PACK)]
         for t in range(PACK):
             cols = slice(t * P, (t + 1) * P)
             nc.tensor.matmul_mx(
@@ -118,11 +121,14 @@ def tile_picked_codermsharm_none_po_kernel(
         settle_rows(plane2, spread2)
         w2 = pick_weights("w2", k2_l)
 
-        sq = [sb("sq%d" % t, [P, S], F32) for t in range(PACK)]
-        sq_own = [sb("sq_own%d" % t, [P, S], F32) for t in range(PACK)]
+        sq = [sb("sq%d" % t, [P, 2 * S], F32) for t in range(PACK)]
+        nc.vector.memset(sq[0][:, S:], 0.0)
+        sq_last = sb("sq_last", [P, S], F32)
+        sq_own = [sq[t + 1][:, S:] for t in range(PACK - 1)] + [sq_last[:]]
         hg = [sb("hg%d" % t, [P, S], F32) for t in range(PACK)]
         ssum = [sb("ssum%d" % t, [P, S], F32) for t in range(PACK)]
-        rinv = [sb("rinv%d" % t, [P, S], F32) for t in range(PACK)]
+        h2 = [sb("h2_%d" % t, [P, 2 * S], F32) for t in range(PACK)]
+        rinv = [h2[t][:, S:] for t in range(PACK)]
         z = [sb("z%d" % c, [P, PACK, HALF], F32) for c in range(2)]
 
         def fetch_z(t, c):
@@ -134,23 +140,29 @@ def tile_picked_codermsharm_none_po_kernel(
             nc.scalar.activation(rinv[t][:, cols], ssum[t][:, cols], ACT.Abs_reciprocal_sqrt, scale=256.0, bias=64.0)
 
         for t in range(PACK):
-            nc.scalar.activation(sq[t][:], h_ps[t][:], ACT.Square, scale=0.0625)
-            nc.scalar.activation(sq_own[t][:], h_ps[t][:], ACT.Square, scale=0.0625)
-            for c in range(2):
-                cols = slice(c * HALF, (c + 1) * HALF)
-                nc.vector.tensor_tensor(ssum[t][:, cols], sq[t][:].indirect(half_of(n1_l, c)), sq_own[t][:, cols], ALU.add)
+            nc.scalar.activation(sq[t][:, 0:S], h_ps[t][:], ACT.Square, scale=0.0625)
+            nc.scalar.activation(sq_own[t], h_ps[t][:], ACT.Square, scale=0.0625)
+            nc.vector.tensor_tensor(ssum[t][:], sq[t][:].indirect(n1_l[:]), sq_own[t], ALU.add)
         for t in range(PACK):
             nc.scalar.activation(hg[t][:], h_ps[t][:], ACT.Copy, scale=gs_t[:, t : t + 1])
             root_of(t, 0)
             fetch_z(t, 0)
-        for t in range(PACK):
+        for t in range(PACK - 1):
             root_of(t, 1)
 
         zq = sb("zq", [P, S], U32)
         zq_bytes = sb("zq_bytes", [P, S], U8)
-        h2_ps = [[psum.tile([P, 2, HALF], F32, name="h2_ps%d%d" % (c, u)) for u in range(2)] for c in range(2)]
-        h2 = [sb("h2_%d" % t, [P, S], F32) for t in range(PACK)]
-        h2_sq = [[sb("h2_sq%d%d" % (c, u), [P, 2, HALF], F32) for u in range(2)] for c in range(2)]
+        pair_ps = {k: psum.tile([P, 2, HALF], F32, name="pair_ps%d%d" % k) for k in [(0, 0), (0, 1), (1, 1)]}
+        h2_ps = {(c, 2 * u + i): pair_ps[c, u][:, i, :] for c, u in pair_ps for i in range(2)}
+        h2_ps[1, 0] = psum.tile([P, HALF], F32, name="lone_ps0", tag="bank3")[:]
+        h2_ps[1, 1] = psum.tile([P, HALF], F32, name="lone_ps1")[:]
+        h2_sq = [sb("h2_sq%d" % u, [P, 2, S], F32) for u in range(2)]
+
+        def square_h2(c, u):
+            nc.scalar.activation(h2_sq[u][:, :, c * HALF : (c + 1) * HALF], pair_ps[c, u][:], ACT.Square, scale=0.0625)
+
+        def square_lone(t):
+            nc.scalar.activation(h2_sq[0][:, t, HALF:S], h2_ps[1, t], ACT.Square, scale=0.0625)
 
         def second_layer(c, z_bf):
             cols = slice(c * HALF, (c + 1) * HALF)
@@ -158,89 +170,129 @@ def tile_picked_codermsharm_none_po_kernel(
             for t in range(PACK):
                 rows = slice(t * P, (t + 1) * P)
                 nc.tensor.matmul_mx(
-                    out=h2_ps[c][t // 2][:, t % 2, :], lhsT=w2[:, rows].bitcast(FP8X4), lhsT_scale=plane2[:, rows],
+                    out=h2_ps[c, t], lhsT=w2[:, rows].bitcast(FP8X4), lhsT_scale=plane2[:, rows],
                     rhs=zq[:, cols].bitcast(FP8X4), rhs_scale=zq_bytes[:, cols], start=True, stop=True,
                 )
 
         def h2_out(c, t):
             cols = slice(c * HALF, (c + 1) * HALF)
             if c == 0:
-                nc.vector.tensor_scalar(h2[t][:, cols], h2_ps[c][t // 2][:, t % 2, :], 0.0625, None, ALU.mult)
+                nc.vector.tensor_scalar(h2[t][:, cols], h2_ps[c, t], 0.0625, None, ALU.mult)
             else:
-                nc.scalar.activation(h2[t][:, cols], h2_ps[c][t // 2][:, t % 2, :], ACT.Copy, scale=0.0625)
+                nc.scalar.activation(h2[t][:, cols], h2_ps[c, t], ACT.Copy, scale=0.0625)
 
         z_bf = [sb("z_bf%d" % c, [P, HALF, PACK], BF16) for c in range(2)]
-        interleave(nc.scalar.copy, z_bf[0], z[0])
+        interleave(nc.scalar.copy, z_bf[0], z[0][:])
+        root_of(PACK - 1, 1)
         for t in range(PACK - 1):
             fetch_z(t, 1)
         second_layer(0, z_bf[0])
         fetch_z(PACK - 1, 1)
-        interleave(nc.vector.tensor_copy, z_bf[1], z[1])
+        for u in range(2):
+            square_h2(0, u)
+        interleave(nc.vector.tensor_copy, z_bf[1], z[1][:])
         h2_out(0, 0)
         second_layer(1, z_bf[1])
         for t in range(1, PACK):
             h2_out(0, t)
-        nc.scalar.activation(h2_sq[0][0][:], h2_ps[0][0][:], ACT.Square, scale=0.0625)
-        for t in range(PACK):
-            h2_out(1, t)
-        nc.scalar.activation(h2_sq[0][1][:], h2_ps[0][1][:], ACT.Square, scale=0.0625)
 
-        units = [(c, u) for c in range(2) for u in range(2)]
-        pa = {k: sb("pa%d%d" % k, [P, 2, HALF], F32) for k in units}
-        pa_sq = {k: sb("pa_sq%d%d" % k, [P, 2, HALF], F32) for k in units}
-        den = {k: sb("den%d%d" % k, [P, 2, HALF], F32) for k in units}
-        root = {k: sb("root%d%d" % k, [P, 2, HALF], F32) for k in units}
-        inv = {k: sb("inv%d%d" % k, [P, 2, HALF], F32) for k in units}
-        num = {k: sb("num%d%d" % k, [P, 2, HALF], F32) for k in units}
-        y = [sb("y%d" % c, [P, PACK, HALF], F32) for c in range(2)]
+        pa = [sb("pa%d" % t, [P, S], F32) for t in range(PACK)]
+        pa_sq = [sb("pa_sq%d" % t, [P, S], F32) for t in range(PACK)]
+        root = [sb("root%d" % t, [P, S], F32) for t in range(PACK)]
+        inv = [sb("inv%d" % t, [P, S], F32) for t in range(PACK)]
+        num = {}
+        den = {}
+        y = sb("y", [P, PACK, S], F32)
         y_bf = [sb("y_bf%d" % c, [P, HALF, PACK], BF16) for c in range(2)]
         yq = sb("yq", [P, S], U32)
         yq_bytes = sb("yq_bytes", [P, S], U8)
         out_rows = out_0.rearrange("(p t) c -> p t c", t=PACK)
         out_words = out_1[0].rearrange("p n t -> p (n t)").bitcast(I32)
 
-        def fetch(k):
-            c, u = k
-            for i in range(2):
-                nc.vector.tensor_copy(pa[k][:, i, :], h2[2 * u + i][:].indirect(half_of(n3_l, c)))
-            nc.scalar.activation(pa_sq[k][:], pa[k][:], ACT.Square)
-            if c == 1:
-                nc.scalar.activation(h2_sq[c][u][:], h2_ps[c][u][:], ACT.Square, scale=0.0625)
+        def fetch(t):
+            nc.vector.tensor_copy(pa[t][:], h2[t][:].indirect(n3_l[:]))
+            nc.scalar.activation(pa_sq[t][:], pa[t][:], ACT.Square)
 
-        def middle(k):
-            c, u = k
-            nc.vector.tensor_tensor(den[k][:], pa_sq[k][:], h2_sq[c][u][:], ALU.add)
-            nc.scalar.activation(root[k][:], den[k][:], ACT.Abs_reciprocal_sqrt, bias=0.5)
-            nc.scalar.activation(inv[k][:], root[k][:], ACT.Square)
-            nc.vector.scalar_tensor_tensor(num[k][:], h2_ps[c][u][:], 0.125, pa[k][:], ALU.mult, ALU.mult)
+        def numerator(t):
+            num[t] = keep.tile([P, S], F32, name="num%d" % t, tag="pa_sq%d" % t, align_bytes=64)
+            nc.vector.tensor_tensor(num[t][:], h2[t][:, 0:S], pa[t][:], ALU.mult)
 
-        def finish(k):
-            c, u = k
-            cols = slice(c * HALF, (c + 1) * HALF)
-            nc.vector.tensor_tensor(y[c][:, 2 * u : 2 * u + 2, :], num[k][:], inv[k][:], ALU.mult)
-            nc.sync.dma_start(out_rows[:, 2 * u : 2 * u + 2, cols], y[c][:, 2 * u : 2 * u + 2, :])
+        def den_by_tensor(t):
+            den[t] = psum.tile([P, S], F32, name="den_ps%d" % t, tag="bank%d" % t)
+            for j in range(S // P):
+                cols = slice(j * P, (j + 1) * P)
+                nc.tensor.matmul(den[t][:, cols], h2_sq[t // 2][:, t % 2, cols], ident[:], start=True, stop=False, is_transpose=True)
+                nc.tensor.matmul(den[t][:, cols], pa_sq[t][:, cols], ident[:], start=False, stop=True, is_transpose=True)
+
+        def den_by_vector(t):
+            den[t] = sb("den%d" % t, [P, S], F32)
+            nc.vector.tensor_tensor(den[t][:], pa_sq[t][:], h2_sq[t // 2][:, t % 2, :], ALU.add)
+
+        def root_den(t):
+            nc.scalar.activation(root[t][:], den[t][:], ACT.Abs_reciprocal_sqrt, scale=0.5, bias=0.25)
+
+        def invert(t):
+            nc.scalar.activation(inv[t][:], root[t][:], ACT.Square)
+
+        def turn_back(t):
+            turned = psum.tile([P, S], F32, name="inv_ps%d" % t, tag="bank%d" % (2 + t))
+            for j in range(S // P):
+                cols = slice(j * P, (j + 1) * P)
+                nc.tensor.transpose(turned[:, cols], inv[t][:, cols], ident[:])
+            inv[t] = turned
+
+        def finish(t, cols):
+            nc.vector.tensor_tensor(y[:, t, cols], num[t][:, cols], inv[t][:, cols], ALU.mult)
+
+        def store(t):
+            nc.sync.dma_start(out_rows[:, t, :], y[:, t, :])
 
         def hand_on(c):
             cols = slice(c * HALF, (c + 1) * HALF)
             nc.vector.quantize_mx(out=yq[:, cols].bitcast(FP8X4), scales=yq_bytes[:, cols], in_=y_bf[c][:].rearrange("p c t -> p (c t)"))
             nc.sync.dma_start(out_words[:, cols], yq[:, cols].bitcast(I32))
 
-        fetch(units[0])
-        fetch(units[1])
-        middle(units[0])
-        fetch(units[2])
-        middle(units[1])
-        finish(units[0])
-        fetch(units[3])
-        middle(units[2])
-        finish(units[1])
-        middle(units[3])
-        interleave(nc.scalar.copy, y_bf[0], y[0])
-        finish(units[2])
-        finish(units[3])
-        hand_on(0)
-        interleave(nc.vector.tensor_copy, y_bf[1], y[1])
+        for t in range(PACK):
+            h2_out(1, t)
+        square_lone(0)
+        square_lone(1)
+        fetch(0)
+        den_by_tensor(0)
+        square_h2(1, 1)
+        fetch(1)
+        den_by_tensor(1)
+        fetch(2)
+        root_den(0)
+        fetch(3)
+        invert(0)
+        turn_back(0)
+        den_by_vector(2)
+        root_den(1)
+        numerator(0)
+        den_by_vector(3)
+        invert(1)
+        root_den(2)
+        turn_back(1)
+        numerator(1)
+        root_den(3)
+        invert(2)
+        invert(3)
+        whole = slice(0, S)
+        finish(0, whole)
+        store(0)
+        numerator(2)
+        finish(1, whole)
+        store(1)
+        numerator(3)
+        finish(2, whole)
+        store(2)
+        for c in range(2):
+            finish(3, slice(c * HALF, (c + 1) * HALF))
+        store(3)
+        interleave(nc.scalar.copy, y_bf[0], y[:, :, 0:HALF])
+        interleave(nc.vector.tensor_copy, y_bf[1], y[:, :, HALF:S])
         hand_on(1)
+        hand_on(0)
         for q in range(4):
             queue = nc.sync if q % 2 == 0 else nc.scalar
             queue.dma_start(out_2[0, 4 * q : 4 * q + 4, :].bitcast(I32), yq_bytes[32 * q : 32 * q + 4, :].bitcast(I32))

@@ -18,6 +18,8 @@ PACK = 4
 K, T, S, G, H = 512, 1024, 512, 2048, 512
 HALF = S // 2
 LANES = 16
+Z_SCALAR = 88
+Y_SCALAR = 232
 FLOPS = 2 * 2 * K * H * S
 
 
@@ -42,7 +44,7 @@ def tile_picked_codermsharm_none_po_kernel(
 
         d_bytes = sb("d_bytes", [P, G], U8)
         x_bytes = sb("x_bytes", [P, T], U8)
-        nc.gpsimd.memset(d_bytes[:].bitcast(I32), 0)
+        nc.vector.memset(d_bytes[:].bitcast(I32), 0)
         nc.vector.memset(x_bytes[:].bitcast(I32), 0)
 
         warm_in = sb("warm_in", [P, 1], F32)
@@ -54,23 +56,24 @@ def tile_picked_codermsharm_none_po_kernel(
         offs_l = load_list("offs_l", offs)
         nc.sync.dma_start(d_bytes[0:P:8, :].bitcast(I32), d_scales[0].bitcast(I32))
         nc.sync.dma_start(x_bytes[0:P:8, :].bitcast(I32), x_scales[0].bitcast(I32))
+        n1_l = load_list("n1_l", n1)
+        n2_l = load_list("n2_l", n2)
         x_tab = sb("x_tab", [P, T], U32)
         d_tab = sb("d_tab", [P, G], U32)
         nc.sync.dma_start(x_tab[:].bitcast(I32), x_words[0].rearrange("p n t -> p (n t)").bitcast(I32))
         nc.sync.dma_start(d_tab[:].bitcast(I32), d_words[0].rearrange("p n t -> p (n t)").bitcast(I32))
-        n1_l = load_list("n1_l", n1)
+        n3_l = load_list("n3_l", n3)
         gs_t = sb("gs_t", [P, PACK], F32)
         nc.sync.dma_start(gs_t[:], gs.rearrange("(p t) o -> p (t o)", t=PACK))
-        n2_l = load_list("n2_l", n2)
-        n3_l = load_list("n3_l", n3)
         k2_l = load_list("k2_l", k2)
 
         plane1 = sb("plane1", [P, H + S], U8)
         plane2 = sb("plane2", [P, H], U8)
-        nc.gpsimd.memset(plane1[:].bitcast(I32), 0)
-        nc.gpsimd.memset(plane2[:].bitcast(I32), 0)
+        nc.vector.memset(plane1[:].bitcast(I32), 0)
+        nc.vector.memset(plane2[:].bitcast(I32), 0)
         ident = sb("ident", [P, P], F32)
-        make_identity(nc, ident[:])
+        nc.vector.memset(ident[:], 0.0)
+        make_identity(nc, ident[:], nomemset=True)
 
         def pick_bytes(name, table, lst):
             got = sb(name, [P, S], U8)
@@ -85,7 +88,7 @@ def tile_picked_codermsharm_none_po_kernel(
                 nc.sync.dma_start(plane[32 * q : 32 * q + 4, :].bitcast(I32), spread[32 * q : 32 * q + 32 : 8, :].bitcast(I32))
 
         def pick_weights(name, lst):
-            got = sb(name + "_got", [P, H], U32)
+            got = keep.tile([P, H], U32, name=name + "_got", tag="picked_words", align_bytes=64)
             nc.vector.tensor_copy(got[:], d_tab[:].indirect(lst[:]))
             dealt = sb(name, [P, H], U32)
             nc.vector.tensor_copy(
@@ -95,7 +98,7 @@ def tile_picked_codermsharm_none_po_kernel(
             return dealt
 
         def interleave(engine_copy, dst, src):
-            engine_copy(dst[:].rearrange("p (c i) t -> p c t i", i=4), src.rearrange("p t (c i) -> p c t i", i=4))
+            engine_copy(dst.rearrange("p (c i) t -> p c t i", i=4), src.rearrange("p t (c i) -> p c t i", i=4))
 
         w1_bytes = pick_bytes("w1_bytes", d_bytes, k1_l)
         xq_bytes = pick_bytes("xq_bytes", x_bytes, offs_l)
@@ -182,7 +185,7 @@ def tile_picked_codermsharm_none_po_kernel(
                 nc.scalar.activation(h2[t][:, cols], h2_ps[c, t], ACT.Copy, scale=0.0625)
 
         z_bf = [sb("z_bf%d" % c, [P, HALF, PACK], BF16) for c in range(2)]
-        interleave(nc.scalar.copy, z_bf[0], z[0][:])
+        interleave(nc.scalar.copy, z_bf[0][:], z[0][:])
         root_of(PACK - 1, 1)
         for t in range(PACK - 1):
             fetch_z(t, 1)
@@ -190,7 +193,8 @@ def tile_picked_codermsharm_none_po_kernel(
         fetch_z(PACK - 1, 1)
         for u in range(2):
             square_h2(0, u)
-        interleave(nc.vector.tensor_copy, z_bf[1], z[1][:])
+        interleave(nc.scalar.copy, z_bf[1][:, 0:Z_SCALAR, :], z[1][:, :, 0:Z_SCALAR])
+        interleave(nc.vector.tensor_copy, z_bf[1][:, Z_SCALAR:, :], z[1][:, :, Z_SCALAR:])
         h2_out(0, 0)
         second_layer(1, z_bf[1])
         for t in range(1, PACK):
@@ -203,7 +207,7 @@ def tile_picked_codermsharm_none_po_kernel(
         num = {}
         den = {}
         y = sb("y", [P, PACK, S], F32)
-        y_bf = [sb("y_bf%d" % c, [P, HALF, PACK], BF16) for c in range(2)]
+        y_bf = sb("y_bf", [P, S, PACK], BF16)
         yq = sb("yq", [P, S], U32)
         yq_bytes = sb("yq_bytes", [P, S], U8)
         out_rows = out_0.rearrange("(p t) c -> p t c", t=PACK)
@@ -218,11 +222,12 @@ def tile_picked_codermsharm_none_po_kernel(
             nc.vector.tensor_tensor(num[t][:], h2[t][:, 0:S], pa[t][:], ALU.mult)
 
         def den_by_tensor(t):
-            den[t] = psum.tile([P, S], F32, name="den_ps%d" % t, tag="bank%d" % t)
-            for j in range(S // P):
-                cols = slice(j * P, (j + 1) * P)
-                nc.tensor.matmul(den[t][:, cols], h2_sq[t // 2][:, t % 2, cols], ident[:], start=True, stop=False, is_transpose=True)
-                nc.tensor.matmul(den[t][:, cols], pa_sq[t][:, cols], ident[:], start=False, stop=True, is_transpose=True)
+            den[t] = psum.tile([P, S], F32, name="den_ps%d" % t, tag="bank%d" % (t % 2))
+            blocks = [slice(j * P, (j + 1) * P) for j in range(S // P)]
+            for cols in blocks:
+                nc.tensor.matmul(den[t][:, cols], h2_sq[t // 2][:, t % 2, cols], ident[:], start=cols is blocks[0], stop=False, is_transpose=True)
+            for cols in blocks:
+                nc.tensor.matmul(den[t][:, cols], pa_sq[t][:, cols], ident[:], start=False, stop=cols is blocks[-1], is_transpose=True)
 
         def den_by_vector(t):
             den[t] = sb("den%d" % t, [P, S], F32)
@@ -235,7 +240,7 @@ def tile_picked_codermsharm_none_po_kernel(
             nc.scalar.activation(inv[t][:], root[t][:], ACT.Square)
 
         def turn_back(t):
-            turned = psum.tile([P, S], F32, name="inv_ps%d" % t, tag="bank%d" % (2 + t))
+            turned = psum.tile([P, S], F32, name="inv_ps%d" % t, tag="bank%d" % (2 + t % 2))
             for j in range(S // P):
                 cols = slice(j * P, (j + 1) * P)
                 nc.tensor.transpose(turned[:, cols], inv[t][:, cols], ident[:])
@@ -249,7 +254,7 @@ def tile_picked_codermsharm_none_po_kernel(
 
         def hand_on(c):
             cols = slice(c * HALF, (c + 1) * HALF)
-            nc.vector.quantize_mx(out=yq[:, cols].bitcast(FP8X4), scales=yq_bytes[:, cols], in_=y_bf[c][:].rearrange("p c t -> p (c t)"))
+            nc.vector.quantize_mx(out=yq[:, cols].bitcast(FP8X4), scales=yq_bytes[:, cols], in_=y_bf[:, cols, :].rearrange("p c t -> p (c t)"))
             nc.sync.dma_start(out_words[:, cols], yq[:, cols].bitcast(I32))
 
         for t in range(PACK):
@@ -261,36 +266,36 @@ def tile_picked_codermsharm_none_po_kernel(
         square_h2(1, 1)
         fetch(1)
         den_by_tensor(1)
-        fetch(2)
         root_den(0)
-        fetch(3)
+        fetch(2)
+        den_by_tensor(2)
         invert(0)
         turn_back(0)
-        den_by_vector(2)
+        fetch(3)
         root_den(1)
         numerator(0)
         den_by_vector(3)
-        invert(1)
         root_den(2)
+        invert(1)
         turn_back(1)
         numerator(1)
-        root_den(3)
         invert(2)
+        turn_back(2)
+        root_den(3)
         invert(3)
-        whole = slice(0, S)
-        finish(0, whole)
+        finish(0, slice(0, S))
         store(0)
         numerator(2)
-        finish(1, whole)
+        finish(1, slice(0, S))
         store(1)
         numerator(3)
-        finish(2, whole)
+        finish(2, slice(0, S))
         store(2)
-        for c in range(2):
-            finish(3, slice(c * HALF, (c + 1) * HALF))
+        for cols in (slice(0, Y_SCALAR), slice(Y_SCALAR, S)):
+            finish(3, cols)
         store(3)
-        interleave(nc.scalar.copy, y_bf[0], y[:, :, 0:HALF])
-        interleave(nc.vector.tensor_copy, y_bf[1], y[:, :, HALF:S])
+        interleave(nc.scalar.copy, y_bf[:, 0:Y_SCALAR, :], y[:, :, 0:Y_SCALAR])
+        interleave(nc.vector.tensor_copy, y_bf[:, Y_SCALAR:S, :], y[:, :, Y_SCALAR:S])
         hand_on(1)
         hand_on(0)
         for q in range(4):

from contextlib import ExitStack

import concourse.mybir as mybir
from concourse.masks import make_identity

F32 = mybir.dt.float32
BF16 = mybir.dt.bfloat16
I32 = mybir.dt.int32
U32 = mybir.dt.uint32
U16 = mybir.dt.uint16
U8 = mybir.dt.uint8
FP8X4 = mybir.dt.float8_e4m3fn_x4
ACT = mybir.ActivationFunctionType
ALU = mybir.AluOpType

P = 128
PACK = 4
K, T, S, G, H = 512, 1024, 512, 2048, 512
HALF = S // 2
LANES = 16
Z_SCALAR = 88
Y_SCALAR = 232
FLOPS = 2 * 2 * K * H * S


def tile_picked_codermsharm_none_po_kernel(
    tc, x_words, x_scales, d_words, d_scales, gs, offs, k1, n1, n2, k2, n3, out_0, out_1, out_2
):
    nc = tc.nc
    with ExitStack() as ctx:
        keep = ctx.enter_context(tc.tile_pool(name="keep", bufs=1))
        psum = ctx.enter_context(tc.psum_pool(name="psum", bufs=1))

        def sb(name, shape, dtype):
            return keep.tile(shape, dtype, name=name, align_bytes=64)

        def load_list(name, src):
            lst = keep.tile([P, S // LANES], U16, name=name)
            nc.sync.dma_start(lst[:], src)
            return lst

        def half_of(lst, c):
            return lst[:, c * HALF // LANES : (c + 1) * HALF // LANES]

        d_bytes = sb("d_bytes", [P, G], U8)
        x_bytes = sb("x_bytes", [P, T], U8)
        nc.vector.memset(d_bytes[:].bitcast(I32), 0)
        nc.vector.memset(x_bytes[:].bitcast(I32), 0)

        warm_in = sb("warm_in", [P, 1], F32)
        warm_out = sb("warm_out", [P, 1], F32)
        nc.vector.memset(warm_in[:], 1.0)
        nc.scalar.activation(warm_out[:], warm_in[:], ACT.Abs_reciprocal_sqrt)

        k1_l = load_list("k1_l", k1)
        offs_l = load_list("offs_l", offs)
        nc.sync.dma_start(d_bytes[0:P:8, :].bitcast(I32), d_scales[0].bitcast(I32))
        nc.sync.dma_start(x_bytes[0:P:8, :].bitcast(I32), x_scales[0].bitcast(I32))
        n1_l = load_list("n1_l", n1)
        n2_l = load_list("n2_l", n2)
        x_tab = sb("x_tab", [P, T], U32)
        d_tab = sb("d_tab", [P, G], U32)
        nc.sync.dma_start(x_tab[:].bitcast(I32), x_words[0].rearrange("p n t -> p (n t)").bitcast(I32))
        nc.sync.dma_start(d_tab[:].bitcast(I32), d_words[0].rearrange("p n t -> p (n t)").bitcast(I32))
        n3_l = load_list("n3_l", n3)
        gs_t = sb("gs_t", [P, PACK], F32)
        nc.sync.dma_start(gs_t[:], gs.rearrange("(p t) o -> p (t o)", t=PACK))
        k2_l = load_list("k2_l", k2)

        plane1 = sb("plane1", [P, H + S], U8)
        plane2 = sb("plane2", [P, H], U8)
        nc.vector.memset(plane1[:].bitcast(I32), 0)
        nc.vector.memset(plane2[:].bitcast(I32), 0)
        ident = sb("ident", [P, P], F32)
        nc.vector.memset(ident[:], 0.0)
        make_identity(nc, ident[:], nomemset=True)

        def pick_bytes(name, table, lst):
            got = sb(name, [P, S], U8)
            nc.vector.tensor_copy(got[:], table[:].indirect(lst[:]))
            return got

        def deal_bytes(dst, got):
            nc.vector.tensor_copy(dst.rearrange("p (t m) -> p t m", t=PACK), got[:].rearrange("p (m t) -> p t m", t=PACK))

        def settle_rows(plane, spread):
            for q in range(4):
                nc.sync.dma_start(plane[32 * q : 32 * q + 4, :].bitcast(I32), spread[32 * q : 32 * q + 32 : 8, :].bitcast(I32))

        def pick_weights(name, lst):
            got = keep.tile([P, H], U32, name=name + "_got", tag="picked_words", align_bytes=64)
            nc.vector.tensor_copy(got[:], d_tab[:].indirect(lst[:]))
            dealt = sb(name, [P, H], U32)
            nc.vector.tensor_copy(
                dealt[:].rearrange("p (t b i) -> p b t i", t=PACK, i=4),
                got[:].rearrange("p (b i t) -> p b t i", t=PACK, i=4),
            )
            return dealt

        def interleave(engine_copy, dst, src):
            engine_copy(dst.rearrange("p (c i) t -> p c t i", i=4), src.rearrange("p t (c i) -> p c t i", i=4))

        w1_bytes = pick_bytes("w1_bytes", d_bytes, k1_l)
        xq_bytes = pick_bytes("xq_bytes", x_bytes, offs_l)
        spread1 = sb("spread1", [P, H + S], U8)
        deal_bytes(spread1[:, 0:H], w1_bytes)
        nc.vector.tensor_copy(spread1[:, H : H + S].bitcast(I32), xq_bytes[:].bitcast(I32))
        settle_rows(plane1, spread1)
        xq = sb("xq", [P, S], U32)
        nc.vector.tensor_copy(xq[:], x_tab[:].indirect(offs_l[:]))
        w1 = pick_weights("w1", k1_l)

        h_ps = [psum.tile([P, S], F32, name="h_ps%d" % t, tag="bank%d" % t) for t in range(PACK)]
        for t in range(PACK):
            cols = slice(t * P, (t + 1) * P)
            nc.tensor.matmul_mx(
                out=h_ps[t][:], lhsT=w1[:, cols].bitcast(FP8X4), lhsT_scale=plane1[:, cols],
                rhs=xq[:].bitcast(FP8X4), rhs_scale=plane1[:, H : H + S], start=True, stop=True,
            )

        w2_bytes = pick_bytes("w2_bytes", d_bytes, k2_l)
        spread2 = sb("spread2", [P, H], U8)
        deal_bytes(spread2[:], w2_bytes)
        settle_rows(plane2, spread2)
        w2 = pick_weights("w2", k2_l)

        sq = [sb("sq%d" % t, [P, 2 * S], F32) for t in range(PACK)]
        nc.vector.memset(sq[0][:, S:], 0.0)
        sq_last = sb("sq_last", [P, S], F32)
        sq_own = [sq[t + 1][:, S:] for t in range(PACK - 1)] + [sq_last[:]]
        hg = [sb("hg%d" % t, [P, S], F32) for t in range(PACK)]
        ssum = [sb("ssum%d" % t, [P, S], F32) for t in range(PACK)]
        h2 = [sb("h2_%d" % t, [P, 2 * S], F32) for t in range(PACK)]
        rinv = [h2[t][:, S:] for t in range(PACK)]
        z = [sb("z%d" % c, [P, PACK, HALF], F32) for c in range(2)]

        def fetch_z(t, c):
            cols = slice(c * HALF, (c + 1) * HALF)
            nc.vector.tensor_tensor(z[c][:, t, :], hg[t][:].indirect(half_of(n2_l, c)), rinv[t][:, cols], ALU.mult)

        def root_of(t, c):
            cols = slice(c * HALF, (c + 1) * HALF)
            nc.scalar.activation(rinv[t][:, cols], ssum[t][:, cols], ACT.Abs_reciprocal_sqrt, scale=256.0, bias=64.0)

        for t in range(PACK):
            nc.scalar.activation(sq[t][:, 0:S], h_ps[t][:], ACT.Square, scale=0.0625)
            nc.scalar.activation(sq_own[t], h_ps[t][:], ACT.Square, scale=0.0625)
            nc.vector.tensor_tensor(ssum[t][:], sq[t][:].indirect(n1_l[:]), sq_own[t], ALU.add)
        for t in range(PACK):
            nc.scalar.activation(hg[t][:], h_ps[t][:], ACT.Copy, scale=gs_t[:, t : t + 1])
            root_of(t, 0)
            fetch_z(t, 0)
        for t in range(PACK - 1):
            root_of(t, 1)

        zq = sb("zq", [P, S], U32)
        zq_bytes = sb("zq_bytes", [P, S], U8)
        pair_ps = {k: psum.tile([P, 2, HALF], F32, name="pair_ps%d%d" % k) for k in [(0, 0), (0, 1), (1, 1)]}
        h2_ps = {(c, 2 * u + i): pair_ps[c, u][:, i, :] for c, u in pair_ps for i in range(2)}
        h2_ps[1, 0] = psum.tile([P, HALF], F32, name="lone_ps0", tag="bank3")[:]
        h2_ps[1, 1] = psum.tile([P, HALF], F32, name="lone_ps1")[:]
        h2_sq = [sb("h2_sq%d" % u, [P, 2, S], F32) for u in range(2)]

        def square_h2(c, u):
            nc.scalar.activation(h2_sq[u][:, :, c * HALF : (c + 1) * HALF], pair_ps[c, u][:], ACT.Square, scale=0.0625)

        def square_lone(t):
            nc.scalar.activation(h2_sq[0][:, t, HALF:S], h2_ps[1, t], ACT.Square, scale=0.0625)

        def second_layer(c, z_bf):
            cols = slice(c * HALF, (c + 1) * HALF)
            nc.vector.quantize_mx(out=zq[:, cols].bitcast(FP8X4), scales=zq_bytes[:, cols], in_=z_bf[:].rearrange("p c t -> p (c t)"))
            for t in range(PACK):
                rows = slice(t * P, (t + 1) * P)
                nc.tensor.matmul_mx(
                    out=h2_ps[c, t], lhsT=w2[:, rows].bitcast(FP8X4), lhsT_scale=plane2[:, rows],
                    rhs=zq[:, cols].bitcast(FP8X4), rhs_scale=zq_bytes[:, cols], start=True, stop=True,
                )

        def h2_out(c, t):
            cols = slice(c * HALF, (c + 1) * HALF)
            if c == 0:
                nc.vector.tensor_scalar(h2[t][:, cols], h2_ps[c, t], 0.0625, None, ALU.mult)
            else:
                nc.scalar.activation(h2[t][:, cols], h2_ps[c, t], ACT.Copy, scale=0.0625)

        z_bf = [sb("z_bf%d" % c, [P, HALF, PACK], BF16) for c in range(2)]
        interleave(nc.scalar.copy, z_bf[0][:], z[0][:])
        root_of(PACK - 1, 1)
        for t in range(PACK - 1):
            fetch_z(t, 1)
        second_layer(0, z_bf[0])
        fetch_z(PACK - 1, 1)
        for u in range(2):
            square_h2(0, u)
        interleave(nc.scalar.copy, z_bf[1][:, 0:Z_SCALAR, :], z[1][:, :, 0:Z_SCALAR])
        interleave(nc.vector.tensor_copy, z_bf[1][:, Z_SCALAR:, :], z[1][:, :, Z_SCALAR:])
        h2_out(0, 0)
        second_layer(1, z_bf[1])
        for t in range(1, PACK):
            h2_out(0, t)

        pa = [sb("pa%d" % t, [P, S], F32) for t in range(PACK)]
        pa_sq = [sb("pa_sq%d" % t, [P, S], F32) for t in range(PACK)]
        root = [sb("root%d" % t, [P, S], F32) for t in range(PACK)]
        inv = [sb("inv%d" % t, [P, S], F32) for t in range(PACK)]
        num = {}
        den = {}
        y = sb("y", [P, PACK, S], F32)
        y_bf = sb("y_bf", [P, S, PACK], BF16)
        yq = sb("yq", [P, S], U32)
        yq_bytes = sb("yq_bytes", [P, S], U8)
        out_rows = out_0.rearrange("(p t) c -> p t c", t=PACK)
        out_words = out_1[0].rearrange("p n t -> p (n t)").bitcast(I32)

        def fetch(t):
            nc.vector.tensor_copy(pa[t][:], h2[t][:].indirect(n3_l[:]))
            nc.scalar.activation(pa_sq[t][:], pa[t][:], ACT.Square)

        def numerator(t):
            num[t] = keep.tile([P, S], F32, name="num%d" % t, tag="pa_sq%d" % t, align_bytes=64)
            nc.vector.tensor_tensor(num[t][:], h2[t][:, 0:S], pa[t][:], ALU.mult)

        def den_by_tensor(t):
            den[t] = psum.tile([P, S], F32, name="den_ps%d" % t, tag="bank%d" % (t % 2))
            blocks = [slice(j * P, (j + 1) * P) for j in range(S // P)]
            for cols in blocks:
                nc.tensor.matmul(den[t][:, cols], h2_sq[t // 2][:, t % 2, cols], ident[:], start=cols is blocks[0], stop=False, is_transpose=True)
            for cols in blocks:
                nc.tensor.matmul(den[t][:, cols], pa_sq[t][:, cols], ident[:], start=False, stop=cols is blocks[-1], is_transpose=True)

        def den_by_vector(t):
            den[t] = sb("den%d" % t, [P, S], F32)
            nc.vector.tensor_tensor(den[t][:], pa_sq[t][:], h2_sq[t // 2][:, t % 2, :], ALU.add)

        def root_den(t):
            nc.scalar.activation(root[t][:], den[t][:], ACT.Abs_reciprocal_sqrt, scale=0.5, bias=0.25)

        def invert(t):
            nc.scalar.activation(inv[t][:], root[t][:], ACT.Square)

        def turn_back(t):
            turned = psum.tile([P, S], F32, name="inv_ps%d" % t, tag="bank%d" % (2 + t % 2))
            for j in range(S // P):
                cols = slice(j * P, (j + 1) * P)
                nc.tensor.transpose(turned[:, cols], inv[t][:, cols], ident[:])
            inv[t] = turned

        def finish(t, cols):
            nc.vector.tensor_tensor(y[:, t, cols], num[t][:, cols], inv[t][:, cols], ALU.mult)

        def store(t):
            nc.sync.dma_start(out_rows[:, t, :], y[:, t, :])

        def hand_on(c):
            cols = slice(c * HALF, (c + 1) * HALF)
            nc.vector.quantize_mx(out=yq[:, cols].bitcast(FP8X4), scales=yq_bytes[:, cols], in_=y_bf[:, cols, :].rearrange("p c t -> p (c t)"))
            nc.sync.dma_start(out_words[:, cols], yq[:, cols].bitcast(I32))

        for t in range(PACK):
            h2_out(1, t)
        square_lone(0)
        square_lone(1)
        fetch(0)
        den_by_tensor(0)
        square_h2(1, 1)
        fetch(1)
        den_by_tensor(1)
        root_den(0)
        fetch(2)
        den_by_tensor(2)
        invert(0)
        turn_back(0)
        fetch(3)
        root_den(1)
        numerator(0)
        den_by_vector(3)
        root_den(2)
        invert(1)
        turn_back(1)
        numerator(1)
        invert(2)
        turn_back(2)
        root_den(3)
        invert(3)
        finish(0, slice(0, S))
        store(0)
        numerator(2)
        finish(1, slice(0, S))
        store(1)
        numerator(3)
        finish(2, slice(0, S))
        store(2)
        for cols in (slice(0, Y_SCALAR), slice(Y_SCALAR, S)):
            finish(3, cols)
        store(3)
        interleave(nc.scalar.copy, y_bf[:, 0:Y_SCALAR, :], y[:, :, 0:Y_SCALAR])
        interleave(nc.vector.tensor_copy, y_bf[:, Y_SCALAR:S, :], y[:, :, Y_SCALAR:S])
        hand_on(1)
        hand_on(0)
        for q in range(4):
            queue = nc.sync if q % 2 == 0 else nc.scalar
            queue.dma_start(out_2[0, 4 * q : 4 * q + 4, :].bitcast(I32), yq_bytes[32 * q : 32 * q + 4, :].bitcast(I32))
